import numpy as np
import ml_dtypes


def mxq(x, axis, fmt="e4m3"):
    dtype, down = {"e4m3": (ml_dtypes.float8_e4m3fn, 7), "e5m2": (ml_dtypes.float8_e5m2, 14)}[fmt]
    v = np.moveaxis(np.asarray(x, np.float32).astype(ml_dtypes.bfloat16).astype(np.float64), axis, -1)
    blocks = v.reshape(v.shape[:-1] + (-1, 32))
    amax = np.abs(blocks).max(-1, keepdims=True)
    byte = np.maximum(np.where(amax > 0, np.frexp(amax)[1] - 1 + 127, 0) - down, 1)
    scale = np.exp2(byte - 127.0)
    codes = (blocks / scale).astype(np.float32).astype(dtype).astype(np.float64)
    return np.moveaxis((codes * scale).reshape(v.shape), -1, axis)


WIDE = False


def mx_kscale(k):
    if not WIDE:
        return np.ones(k)
    levels = np.array([30, -30])
    if k % 512:
        return np.exp2(np.random.permutation(np.resize(levels, k // 32))).repeat(32)
    a = np.empty((k // 512, 16))
    for p in range(k // 512):
        a[p, :8] = np.random.permutation(np.resize(levels, 8))
        for g in range(8):
            far = levels[np.abs(levels - a[p, g]) >= 10]
            a[p, g + 8] = far[np.random.randint(len(far))]
    return np.exp2(a.ravel()).repeat(32)


def f64(x):
    return np.asarray(x).astype(np.float64)


def striped(idx):
    return np.tile(np.asarray(idx).reshape(-1, 16).T, (8, 1)).astype(np.uint16)


def unstriped(offs):
    return offs[:16].T.reshape(-1).astype(np.int64)


T, K, N, J = 1024, 512, 1024, 512


def setup_inputs():
    n = np.random.standard_normal
    idx = np.random.permutation(N)[:J]
    ft = mx_kscale(T)
    return {
        "xt": (n((T, K)) * ft[:, None]).astype(np.float32),
        "g": (n((T, N)) * np.exp(0.5 * n((T, 1))) / ft[:, None]).astype(np.float32),
        "mom": (1.0 * n((K, N))).astype(np.float32),
        "offs": striped(idx),
    }


def reference(xt, g, mom, offs):
    idx = unstriped(offs)
    xtq = mxq(f64(xt), 0, "e4m3")
    gidxq = mxq(f64(g)[:, idx], 0, "e5m2")
    w = xtq.T @ gidxq
    d = 0.03 * w - 0.1 * f64(mom)[:, idx]
    p = np.zeros((K, N))
    p[:, idx] = d
    y = f64(mom) + p
    return y

@@ -1,0 +1,185 @@
+from contextlib import ExitStack
+
+import concourse.mybir as mybir
+from concourse.masks import make_identity
+
+T, K, N, J = 1024, 512, 1024, 512
+FLOPS = 2 * T * K * J
+
+F32 = mybir.dt.float32
+BF16 = mybir.dt.bfloat16
+U32 = mybir.dt.uint32
+U16 = mybir.dt.uint16
+U8 = mybir.dt.uint8
+E4M3 = mybir.dt.float8_e4m3fn_x4
+E5M2 = mybir.dt.float8_e5m2_x4
+COPY = mybir.ActivationFunctionType.Copy
+MULT = mybir.AluOpType.mult
+ADD = mybir.AluOpType.add
+
+P = 128
+PACK = 4
+T_PASS = P * PACK
+PASSES = T // T_PASS
+BLOCKS = K // P
+HALF = 512
+
+
+def tile_list_sparse_momentum_kernel(tc, xt, g, mom, offs, out):
+    nc = tc.nc
+    with ExitStack() as ctx:
+        keep = ctx.enter_context(tc.tile_pool(name="keep", bufs=1))
+        ring = ctx.enter_context(tc.tile_pool(name="ring", bufs=2))
+        psum = ctx.enter_context(tc.psum_pool(name="psum", bufs=1))
+
+        offsets = keep.tile([P, J // 16], U16, name="offsets")
+        nc.sync.dma_start(offsets[:], offs)
+
+        g_rows = g.rearrange("(a p j) n -> a p j n", p=P, j=PACK)
+        x_rows = xt.rearrange("(a p j) k -> a p j k", p=P, j=PACK)
+
+        mom_win = [keep.tile([P, 2 * N], F32, name=f"mom_win{b}") for b in range(BLOCKS)]
+        pages = [keep.tile([P, N], F32, name=f"page{i}") for i in range(2)]
+        ident = keep.tile([P, P], F32, name="ident")
+        make_identity(nc, ident[:])
+        for b in range(BLOCKS):
+            engine = nc.vector if b < 2 else nc.gpsimd
+            engine.memset(mom_win[b][:, N:].bitcast(U32), 0)
+        for page in pages:
+            nc.vector.memset(page[:].bitcast(U32), 0)
+        banks = [psum.tile([P, HALF], F32, name=f"bank{i}") for i in range(6)]
+
+        def load_g(a, u, c0, c1):
+            raw = keep.tile([P, 2, c1 - c0], F32, name=f"g_raw{a}{u}_{c0}")
+            nc.sync.dma_start(raw[:], g_rows[a, :, 2 * u : 2 * u + 2, c0:c1])
+            return raw
+
+        def load_x(a, c0, c1):
+            raw = keep.tile([P, PACK, c1 - c0], F32, name=f"x_raw{a}_{c0}", align_bytes=64)
+            nc.sync.dma_start(raw[:], x_rows[a, :, :, c0:c1])
+            return raw
+
+        def load_mom(b):
+            nc.sync.dma_start(mom_win[b][:, :N], mom[b * P : (b + 1) * P, :])
+
+        cuts = {(0, 0): (0, 512, 1024), (0, 1): (0, 512, 1024), (1, 0): (0, 512, 1024), (1, 1): (0, 512, 768, 1024)}
+        g_raw = {}
+        x_raw = {}
+        for a in range(PASSES):
+            for u in range(2):
+                c = cuts[(a, u)]
+                g_raw[(a, u)] = [(c0, c1, load_g(a, u, c0, c1)) for c0, c1 in zip(c, c[1:])]
+        for aa in range(PASSES):
+            x_raw[(0, aa)] = load_x(aa, 0, P)
+        load_mom(0)
+        for aa in range(PASSES):
+            x_raw[(1, aa)] = load_x(aa, P, 2 * P)
+        x_rest = [load_x(0, 2 * P, K)]
+        load_mom(1)
+        x_rest.append(load_x(1, 2 * P, K))
+        load_mom(2)
+        load_mom(3)
+
+        g_scales = [keep.tile([P, J], U8, name=f"g_scales{a}", align_bytes=64) for a in range(PASSES)]
+        x_grouped = [keep.tile([P, PASSES * P * PACK], BF16, name=f"x_grouped{b}", align_bytes=64) for b in range(BLOCKS)]
+        x_codes = [keep.tile([P, PASSES * P], U32, name=f"x_codes{b}", align_bytes=64) for b in range(BLOCKS)]
+        x_scales = [keep.tile([P, PASSES * P], U8, name=f"x_scales{b}", align_bytes=64) for b in range(BLOCKS)]
+
+        def x_source(b, a):
+            if b < 2:
+                return x_raw[(b, a)][:]
+            return x_rest[a][:, :, (b - 2) * P : (b - 1) * P]
+
+        def group_x(b):
+            for a in range(PASSES):
+                dst = x_grouped[b][:, a * T_PASS : (a + 1) * T_PASS].rearrange("p (c i j) -> p c j i", i=4, j=PACK)
+                src = x_source(b, a).rearrange("p j (c i) -> p c j i", i=4)
+                nc.scalar.activation(dst, src, COPY)
+
+        def quantize_x(b, a0, a1):
+            nc.vector.quantize_mx(
+                out=x_codes[b][:, a0 * P : a1 * P].bitcast(E4M3),
+                scales=x_scales[b][:, a0 * P : a1 * P],
+                in_=x_grouped[b][:, a0 * T_PASS : a1 * T_PASS],
+            )
+
+        g_codes = []
+        for a in range(PASSES):
+            picked = keep.tile([P, J * PACK], BF16, name=f"g_picked{a}", align_bytes=64)
+            picked_words = picked[:].bitcast(U32).rearrange("p (j u) -> p j u", u=2)
+            for u in range(2):
+                window = keep.tile([P, N], U32, name=f"g_pairs{a}{u}")
+                pairs = window[:].bitcast(BF16).rearrange("p (n e) -> p n e", e=2)
+                for c0, c1, raw in g_raw[(a, u)]:
+                    nc.scalar.activation(pairs[:, c0:c1, :], raw[:].rearrange("p e n -> p n e"), COPY)
+                nc.vector.tensor_copy(picked_words[:, :, u], window[:].indirect(offsets[:]))
+            if a == PASSES - 1:
+                group_x(0)
+                quantize_x(0, 0, 1)
+            g_codes.append(keep.tile([P, J], U32, name="x_raw0_0" if a == PASSES - 1 else "g_codes0", align_bytes=64))
+            nc.vector.quantize_mx(out=g_codes[a][:].bitcast(E5M2), scales=g_scales[a][:], in_=picked[:])
+        quantize_x(0, 1, 2)
+
+        def product(b):
+            w = banks[b]
+            for a in range(PASSES):
+                cols = slice(a * P, (a + 1) * P)
+                nc.tensor.matmul_mx(
+                    out=w[:],
+                    lhsT=x_codes[b][:, cols].bitcast(E4M3),
+                    lhsT_scale=x_scales[b][:, cols],
+                    rhs=g_codes[a][:].bitcast(E5M2),
+                    rhs_scale=g_scales[a][:],
+                    start=(a == 0),
+                    stop=(a == PASSES - 1),
+                )
+            w_part = keep.tile([P, J], F32, name=f"x_raw1_{2 * P}" if b == 1 else f"w_part{b}", align_bytes=64)
+            nc.scalar.activation(w_part[:], w[:], COPY, scale=0.03)
+            return w_part
+
+        def pick_mom(b):
+            mom_part = keep.tile([P, J], F32, name=f"mom_part{b}")
+            nc.vector.tensor_scalar(mom_part[:], mom_win[b][:].indirect(offsets[:]), -0.1, 0.0, MULT, ADD)
+            return mom_part
+
+        turned_banks = [(banks[1], banks[2]), (banks[4], banks[5]), (banks[4], banks[5])]
+        back_banks = [(banks[4], banks[5]), (banks[0], banks[3]), (banks[1], banks[2])]
+
+        def sum_on_tensor(b, page):
+            for source, first in ((mom_win[b], True), (page, False)):
+                for h, turned in enumerate(turned_banks[b]):
+                    for i in range(HALF // P):
+                        n0 = h * HALF + i * P
+                        nc.tensor.matmul(turned[:, i * P : (i + 1) * P], source[:, n0 : n0 + P], ident[:],
+                                         start=(first and i == 0), stop=(not first and i == HALF // P - 1),
+                                         is_transpose=True)
+            for h, (turned, back) in enumerate(zip(turned_banks[b], back_banks[b])):
+                turned_sb = ring.tile([P, HALF], F32, name="turned_sb")
+                nc.scalar.copy(turned_sb[:], turned[:])
+                for i in range(HALF // P):
+                    nc.tensor.transpose(back[:, i * P : (i + 1) * P], turned_sb[:, i * P : (i + 1) * P], ident[:])
+                result = keep.tile([P, HALF], F32, name=f"result{b}{h}")
+                nc.scalar.copy(result[:], back[:])
+                nc.scalar.dma_start(out[b * P : (b + 1) * P, h * HALF : (h + 1) * HALF], result[:])
+
+        def sum_on_vector(b, page):
+            for h in range(N // HALF):
+                cols = slice(h * HALF, (h + 1) * HALF)
+                result = keep.tile([P, HALF], F32, name=f"result{b}{h}")
+                nc.vector.tensor_tensor(result[:], mom_win[b][:, cols], page[:, cols], ADD)
+                nc.sync.dma_start(out[b * P : (b + 1) * P, cols], result[:])
+
+        w_parts = [product(0)]
+        for b in range(1, BLOCKS):
+            group_x(b)
+        for b in range(1, BLOCKS):
+            quantize_x(b, 0, PASSES)
+            w_parts.append(product(b))
+        for b in range(BLOCKS):
+            mom_part = pick_mom(b)
+            page = pages[b % 2]
+            nc.vector.tensor_tensor(page[:].indirect(offsets[:]), w_parts[b][:], mom_part[:], ADD)
+            if b + 1 < BLOCKS:
+                sum_on_tensor(b, page)
+            else:
+                sum_on_vector(b, page)

@@ -33,7 +33,6 @@ def tile_list_sparse_momentum_kernel(tc, xt, g, mom, offs, out):
         psum = ctx.enter_context(tc.psum_pool(name="psum", bufs=1))
 
         offsets = keep.tile([P, J // 16], U16, name="offsets")
-        nc.sync.dma_start(offsets[:], offs)
 
         g_rows = g.rearrange("(a p j) n -> a p j n", p=P, j=PACK)
         x_rows = xt.rearrange("(a p j) k -> a p j k", p=P, j=PACK)
@@ -62,23 +61,19 @@ def tile_list_sparse_momentum_kernel(tc, xt, g, mom, offs, out):
         def load_mom(b):
             nc.sync.dma_start(mom_win[b][:, :N], mom[b * P : (b + 1) * P, :])
 
-        cuts = {(0, 0): (0, 512, 1024), (0, 1): (0, 512, 1024), (1, 0): (0, 512, 1024), (1, 1): (0, 512, 768, 1024)}
+        cuts = {(0, 0): (0, 1024), (0, 1): (0, 512, 1024), (1, 0): (0, 512, 1024), (1, 1): (0, 512, 768, 1024)}
         g_raw = {}
-        x_raw = {}
         for a in range(PASSES):
             for u in range(2):
                 c = cuts[(a, u)]
                 g_raw[(a, u)] = [(c0, c1, load_g(a, u, c0, c1)) for c0, c1 in zip(c, c[1:])]
-        for aa in range(PASSES):
-            x_raw[(0, aa)] = load_x(aa, 0, P)
+                if (a, u) == (0, 0):
+                    nc.sync.dma_start(offsets[:], offs)
+        x_first = [load_x(a, 0, P) for a in range(PASSES)]
         load_mom(0)
-        for aa in range(PASSES):
-            x_raw[(1, aa)] = load_x(aa, P, 2 * P)
-        x_rest = [load_x(0, 2 * P, K)]
-        load_mom(1)
-        x_rest.append(load_x(1, 2 * P, K))
-        load_mom(2)
-        load_mom(3)
+        x_rest = [load_x(a, P, K) for a in range(PASSES)]
+        for b in range(1, BLOCKS):
+            load_mom(b)
 
         g_scales = [keep.tile([P, J], U8, name=f"g_scales{a}", align_bytes=64) for a in range(PASSES)]
         x_grouped = [keep.tile([P, PASSES * P * PACK], BF16, name=f"x_grouped{b}", align_bytes=64) for b in range(BLOCKS)]
@@ -86,14 +81,14 @@ def tile_list_sparse_momentum_kernel(tc, xt, g, mom, offs, out):
         x_scales = [keep.tile([P, PASSES * P], U8, name=f"x_scales{b}", align_bytes=64) for b in range(BLOCKS)]
 
         def x_source(b, a):
-            if b < 2:
-                return x_raw[(b, a)][:]
-            return x_rest[a][:, :, (b - 2) * P : (b - 1) * P]
+            if b == 0:
+                return x_first[a][:]
+            return x_rest[a][:, :, (b - 1) * P : b * P]
 
         def group_x(b):
             for a in range(PASSES):
-                dst = x_grouped[b][:, a * T_PASS : (a + 1) * T_PASS].rearrange("p (c i j) -> p c j i", i=4, j=PACK)
-                src = x_source(b, a).rearrange("p j (c i) -> p c j i", i=4)
+                dst = x_grouped[b][:, a * T_PASS : (a + 1) * T_PASS].rearrange("p (c j) -> p c j", j=PACK)
+                src = x_source(b, a).rearrange("p j c -> p c j")
                 nc.scalar.activation(dst, src, COPY)
 
         def quantize_x(b, a0, a1):
@@ -111,7 +106,12 @@ def tile_list_sparse_momentum_kernel(tc, xt, g, mom, offs, out):
                 window = keep.tile([P, N], U32, name=f"g_pairs{a}{u}")
                 pairs = window[:].bitcast(BF16).rearrange("p (n e) -> p n e", e=2)
                 for c0, c1, raw in g_raw[(a, u)]:
-                    nc.scalar.activation(pairs[:, c0:c1, :], raw[:].rearrange("p e n -> p n e"), COPY)
+                    planes = raw[:].rearrange("p e n -> p n e")
+                    if (a, u) == (0, 0):
+                        nc.scalar.activation(pairs[:, :HALF, :], planes[:, :HALF, :], COPY)
+                        nc.vector.tensor_copy(pairs[:, HALF:, :], planes[:, HALF:, :])
+                    else:
+                        nc.scalar.activation(pairs[:, c0:c1, :], planes, COPY)
                 nc.vector.tensor_copy(picked_words[:, :, u], window[:].indirect(offsets[:]))
             if a == PASSES - 1:
                 group_x(0)
@@ -133,7 +133,7 @@ def tile_list_sparse_momentum_kernel(tc, xt, g, mom, offs, out):
                     start=(a == 0),
                     stop=(a == PASSES - 1),
                 )
-            w_part = keep.tile([P, J], F32, name=f"x_raw1_{2 * P}" if b == 1 else f"w_part{b}", align_bytes=64)
+            w_part = keep.tile([P, J], F32, name=f"x_raw1_{P}" if b == 1 else f"w_part{b}", align_bytes=64)
             nc.scalar.activation(w_part[:], w[:], COPY, scale=0.03)
             return w_part
 
@@ -163,9 +163,9 @@ def tile_list_sparse_momentum_kernel(tc, xt, g, mom, offs, out):
                 nc.scalar.dma_start(out[b * P : (b + 1) * P, h * HALF : (h + 1) * HALF], result[:])
 
         def sum_on_vector(b, page):
-            for h in range(N // HALF):
-                cols = slice(h * HALF, (h + 1) * HALF)
-                result = keep.tile([P, HALF], F32, name=f"result{b}{h}")
+            for h in range(4):
+                cols = slice(h * 256, (h + 1) * 256)
+                result = keep.tile([P, 256], F32, name=f"result{b}{h}")
                 nc.vector.tensor_tensor(result[:], mom_win[b][:, cols], page[:, cols], ADD)
                 nc.sync.dma_start(out[b * P : (b + 1) * P, cols], result[:])
 

from contextlib import ExitStack

import concourse.mybir as mybir
from concourse.masks import make_identity

T, K, N, J = 1024, 512, 1024, 512
FLOPS = 2 * T * K * J

F32 = mybir.dt.float32
BF16 = mybir.dt.bfloat16
U32 = mybir.dt.uint32
U16 = mybir.dt.uint16
U8 = mybir.dt.uint8
E4M3 = mybir.dt.float8_e4m3fn_x4
E5M2 = mybir.dt.float8_e5m2_x4
COPY = mybir.ActivationFunctionType.Copy
MULT = mybir.AluOpType.mult
ADD = mybir.AluOpType.add

P = 128
PACK = 4
T_PASS = P * PACK
PASSES = T // T_PASS
BLOCKS = K // P
HALF = 512


def tile_list_sparse_momentum_kernel(tc, xt, g, mom, offs, out):
    nc = tc.nc
    with ExitStack() as ctx:
        keep = ctx.enter_context(tc.tile_pool(name="keep", bufs=1))
        ring = ctx.enter_context(tc.tile_pool(name="ring", bufs=2))
        psum = ctx.enter_context(tc.psum_pool(name="psum", bufs=1))

        offsets = keep.tile([P, J // 16], U16, name="offsets")

        g_rows = g.rearrange("(a p j) n -> a p j n", p=P, j=PACK)
        x_rows = xt.rearrange("(a p j) k -> a p j k", p=P, j=PACK)

        mom_win = [keep.tile([P, 2 * N], F32, name=f"mom_win{b}") for b in range(BLOCKS)]
        pages = [keep.tile([P, N], F32, name=f"page{i}") for i in range(2)]
        ident = keep.tile([P, P], F32, name="ident")
        make_identity(nc, ident[:])
        for b in range(BLOCKS):
            engine = nc.vector if b < 2 else nc.gpsimd
            engine.memset(mom_win[b][:, N:].bitcast(U32), 0)
        for page in pages:
            nc.vector.memset(page[:].bitcast(U32), 0)
        banks = [psum.tile([P, HALF], F32, name=f"bank{i}") for i in range(6)]

        def load_g(a, u, c0, c1):
            raw = keep.tile([P, 2, c1 - c0], F32, name=f"g_raw{a}{u}_{c0}")
            nc.sync.dma_start(raw[:], g_rows[a, :, 2 * u : 2 * u + 2, c0:c1])
            return raw

        def load_x(a, c0, c1):
            raw = keep.tile([P, PACK, c1 - c0], F32, name=f"x_raw{a}_{c0}", align_bytes=64)
            nc.sync.dma_start(raw[:], x_rows[a, :, :, c0:c1])
            return raw

        def load_mom(b):
            nc.sync.dma_start(mom_win[b][:, :N], mom[b * P : (b + 1) * P, :])

        cuts = {(0, 0): (0, 1024), (0, 1): (0, 512, 1024), (1, 0): (0, 512, 1024), (1, 1): (0, 512, 768, 1024)}
        g_raw = {}
        for a in range(PASSES):
            for u in range(2):
                c = cuts[(a, u)]
                g_raw[(a, u)] = [(c0, c1, load_g(a, u, c0, c1)) for c0, c1 in zip(c, c[1:])]
                if (a, u) == (0, 0):
                    nc.sync.dma_start(offsets[:], offs)
        x_first = [load_x(a, 0, P) for a in range(PASSES)]
        load_mom(0)
        x_rest = [load_x(a, P, K) for a in range(PASSES)]
        for b in range(1, BLOCKS):
            load_mom(b)

        g_scales = [keep.tile([P, J], U8, name=f"g_scales{a}", align_bytes=64) for a in range(PASSES)]
        x_grouped = [keep.tile([P, PASSES * P * PACK], BF16, name=f"x_grouped{b}", align_bytes=64) for b in range(BLOCKS)]
        x_codes = [keep.tile([P, PASSES * P], U32, name=f"x_codes{b}", align_bytes=64) for b in range(BLOCKS)]
        x_scales = [keep.tile([P, PASSES * P], U8, name=f"x_scales{b}", align_bytes=64) for b in range(BLOCKS)]

        def x_source(b, a):
            if b == 0:
                return x_first[a][:]
            return x_rest[a][:, :, (b - 1) * P : b * P]

        def group_x(b):
            for a in range(PASSES):
                dst = x_grouped[b][:, a * T_PASS : (a + 1) * T_PASS].rearrange("p (c j) -> p c j", j=PACK)
                src = x_source(b, a).rearrange("p j c -> p c j")
                nc.scalar.activation(dst, src, COPY)

        def quantize_x(b, a0, a1):
            nc.vector.quantize_mx(
                out=x_codes[b][:, a0 * P : a1 * P].bitcast(E4M3),
                scales=x_scales[b][:, a0 * P : a1 * P],
                in_=x_grouped[b][:, a0 * T_PASS : a1 * T_PASS],
            )

        g_codes = []
        for a in range(PASSES):
            picked = keep.tile([P, J * PACK], BF16, name=f"g_picked{a}", align_bytes=64)
            picked_words = picked[:].bitcast(U32).rearrange("p (j u) -> p j u", u=2)
            for u in range(2):
                window = keep.tile([P, N], U32, name=f"g_pairs{a}{u}")
                pairs = window[:].bitcast(BF16).rearrange("p (n e) -> p n e", e=2)
                for c0, c1, raw in g_raw[(a, u)]:
                    planes = raw[:].rearrange("p e n -> p n e")
                    if (a, u) == (0, 0):
                        nc.scalar.activation(pairs[:, :HALF, :], planes[:, :HALF, :], COPY)
                        nc.vector.tensor_copy(pairs[:, HALF:, :], planes[:, HALF:, :])
                    else:
                        nc.scalar.activation(pairs[:, c0:c1, :], planes, COPY)
                nc.vector.tensor_copy(picked_words[:, :, u], window[:].indirect(offsets[:]))
            if a == PASSES - 1:
                group_x(0)
                quantize_x(0, 0, 1)
            g_codes.append(keep.tile([P, J], U32, name="x_raw0_0" if a == PASSES - 1 else "g_codes0", align_bytes=64))
            nc.vector.quantize_mx(out=g_codes[a][:].bitcast(E5M2), scales=g_scales[a][:], in_=picked[:])
        quantize_x(0, 1, 2)

        def product(b):
            w = banks[b]
            for a in range(PASSES):
                cols = slice(a * P, (a + 1) * P)
                nc.tensor.matmul_mx(
                    out=w[:],
                    lhsT=x_codes[b][:, cols].bitcast(E4M3),
                    lhsT_scale=x_scales[b][:, cols],
                    rhs=g_codes[a][:].bitcast(E5M2),
                    rhs_scale=g_scales[a][:],
                    start=(a == 0),
                    stop=(a == PASSES - 1),
                )
            w_part = keep.tile([P, J], F32, name=f"x_raw1_{P}" if b == 1 else f"w_part{b}", align_bytes=64)
            nc.scalar.activation(w_part[:], w[:], COPY, scale=0.03)
            return w_part

        def pick_mom(b):
            mom_part = keep.tile([P, J], F32, name=f"mom_part{b}")
            nc.vector.tensor_scalar(mom_part[:], mom_win[b][:].indirect(offsets[:]), -0.1, 0.0, MULT, ADD)
            return mom_part

        turned_banks = [(banks[1], banks[2]), (banks[4], banks[5]), (banks[4], banks[5])]
        back_banks = [(banks[4], banks[5]), (banks[0], banks[3]), (banks[1], banks[2])]

        def sum_on_tensor(b, page):
            for source, first in ((mom_win[b], True), (page, False)):
                for h, turned in enumerate(turned_banks[b]):
                    for i in range(HALF // P):
                        n0 = h * HALF + i * P
                        nc.tensor.matmul(turned[:, i * P : (i + 1) * P], source[:, n0 : n0 + P], ident[:],
                                         start=(first and i == 0), stop=(not first and i == HALF // P - 1),
                                         is_transpose=True)
            for h, (turned, back) in enumerate(zip(turned_banks[b], back_banks[b])):
                turned_sb = ring.tile([P, HALF], F32, name="turned_sb")
                nc.scalar.copy(turned_sb[:], turned[:])
                for i in range(HALF // P):
                    nc.tensor.transpose(back[:, i * P : (i + 1) * P], turned_sb[:, i * P : (i + 1) * P], ident[:])
                result = keep.tile([P, HALF], F32, name=f"result{b}{h}")
                nc.scalar.copy(result[:], back[:])
                nc.scalar.dma_start(out[b * P : (b + 1) * P, h * HALF : (h + 1) * HALF], result[:])

        def sum_on_vector(b, page):
            for h in range(4):
                cols = slice(h * 256, (h + 1) * 256)
                result = keep.tile([P, 256], F32, name=f"result{b}{h}")
                nc.vector.tensor_tensor(result[:], mom_win[b][:, cols], page[:, cols], ADD)
                nc.sync.dma_start(out[b * P : (b + 1) * P, cols], result[:])

        w_parts = [product(0)]
        for b in range(1, BLOCKS):
            group_x(b)
        for b in range(1, BLOCKS):
            quantize_x(b, 0, PASSES)
            w_parts.append(product(b))
        for b in range(BLOCKS):
            mom_part = pick_mom(b)
            page = pages[b % 2]
            nc.vector.tensor_tensor(page[:].indirect(offsets[:]), w_parts[b][:], mom_part[:], ADD)
            if b + 1 < BLOCKS:
                sum_on_tensor(b, page)
            else:
                sum_on_vector(b, page)
